import numpy as np
import ml_dtypes


def mxq(x, axis, fmt="e4m3"):
    dtype, down = {"e4m3": (ml_dtypes.float8_e4m3fn, 7), "e5m2": (ml_dtypes.float8_e5m2, 14)}[fmt]
    v = np.moveaxis(np.asarray(x, np.float32).astype(ml_dtypes.bfloat16).astype(np.float64), axis, -1)
    blocks = v.reshape(v.shape[:-1] + (-1, 32))
    amax = np.abs(blocks).max(-1, keepdims=True)
    byte = np.maximum(np.where(amax > 0, np.frexp(amax)[1] - 1 + 127, 0) - down, 1)
    scale = np.exp2(byte - 127.0)
    codes = (blocks / scale).astype(np.float32).astype(dtype).astype(np.float64)
    return np.moveaxis((codes * scale).reshape(v.shape), -1, axis)


WIDE = False


def mx_kscale(k):
    if not WIDE:
        return np.ones(k)
    levels = np.array([10, -10, 5, -5, 0])
    if k % 512:
        return np.exp2(np.random.permutation(np.resize(levels, k // 32))).repeat(32)
    a = np.empty((k // 512, 16))
    for p in range(k // 512):
        a[p, :8] = np.random.permutation(np.resize(levels, 8))
        for g in range(8):
            far = levels[np.abs(levels - a[p, g]) >= 10]
            a[p, g + 8] = far[np.random.randint(len(far))]
    return np.exp2(a.ravel()).repeat(32)


def f64(x):
    return np.asarray(x).astype(np.float64)


def striped(idx):
    return np.tile(idx.reshape(-1, 16).T, (8, 1)).astype(np.uint16)


def unstriped(offs):
    return offs[:16].T.reshape(-1).astype(np.int64)


def pack_weight(w):
    k, n = w.shape
    w = f64(np.asarray(w, np.float32).astype(ml_dtypes.bfloat16)).reshape(k // 32, 32, n)
    amax = np.abs(w).max(1)
    byte = np.clip(np.where(amax > 0, np.frexp(amax)[1] - 1 + 127 - 7, 1), 1, 254)
    scaled = (w * np.exp2(127.0 - byte)[:, None, :]).reshape(k, n).astype(np.float32)
    words = np.ascontiguousarray(scaled.reshape(k // 512, 128, 4, n).transpose(0, 1, 3, 2)).astype(ml_dtypes.float8_e4m3fn).view(np.uint8)
    return words, np.ascontiguousarray(byte.astype(np.uint8).reshape(k // 512, 16, n))


def unpack_weight(words, scales):
    g, p, n, _ = words.shape
    vals = np.ascontiguousarray(words).view(ml_dtypes.float8_e4m3fn).astype(np.float64) * np.repeat(np.exp2(scales.astype(np.float64) - 127.0), 8, axis=1)[..., None]
    return vals.transpose(0, 1, 3, 2).reshape(g * 512, n)


def gelu(v):
    return 0.5 * v * (1.0 + np.tanh(np.sqrt(2.0 / np.pi) * (v + 0.044715 * v**3)))


K, T, E, C, N = 1536, 2048, 8, 128, 128


def by_expert(wq, xq):
    return np.concatenate([wq[e].T @ xq[:, e * C:(e + 1) * C] for e in range(E)], axis=1)


def setup_inputs():
    n = np.random.standard_normal
    s = mx_kscale(K)[:, None]
    packed = [pack_weight(m) for m in n((E, K, N)) / np.sqrt(K) / s[None]]
    return {
        "xT": (n((K, T)) * s).astype(np.float32),
        "w_words": np.stack([m[0] for m in packed]),
        "w_scales": np.stack([m[1] for m in packed]),
        "b": (0.3 * n((N, E))).astype(np.float32),
        "gate": np.tile(np.random.uniform(0.2, 1.0, E * C), (N, 1)).astype(np.float32),
        "offs": striped(np.random.permutation(T)[:E * C]),
    }


def reference(xT, w_words, w_scales, b, gate, offs):
    idx = unstriped(offs)
    xq = mxq(f64(xT)[:, idx], 0, "e4m3")
    w = np.stack([unpack_weight(w_words[e], w_scales[e]) for e in range(E)])
    y = by_expert(w, xq)
    y = gelu(y + np.repeat(f64(b), C, axis=1))
    out = np.zeros((N, T))
    out[:, idx] = f64(gate) * y
    return out

@@ -1,0 +1,135 @@
+from contextlib import ExitStack
+
+import concourse.mybir as mybir
+
+K, T, E, C, N = 1536, 2048, 8, 128, 128
+FLOPS = 2 * K * N * E * C
+
+F32 = mybir.dt.float32
+BF16 = mybir.dt.bfloat16
+U32 = mybir.dt.uint32
+I32 = mybir.dt.int32
+U16 = mybir.dt.uint16
+U8 = mybir.dt.uint8
+FP8X4 = mybir.dt.float8_e4m3fn_x4
+GELU = mybir.ActivationFunctionType.Gelu_apprx_tanh
+MULT = mybir.AluOpType.mult
+
+P = 128
+PASSES = K // 512
+S = E * C
+
+CHUNKS = [
+    [(512, 384), (512, 384), (1024, 768)],
+    [(2048, 1600)],
+    [(2048, 1600)],
+    [(2048, 1600)],
+    [(1024, 768), (1024, 768)],
+    [(1024, 768), (512, 320), (256, 96), (256, 96)],
+]
+SLICE = 256
+
+
+def tile_routed_moe_kernel(tc, xT, w_words, w_scales, b, gate, offs, out):
+    nc = tc.nc
+    planes = xT.rearrange("(g p u j) t -> g u p j t", g=PASSES, p=P, u=2, j=2)
+    words_hbm = w_words.rearrange("e a p n r -> p (e a) (n r)")
+    scales_hbm = w_scales.rearrange("e a (q i) n -> i q (e a) n", i=4)
+
+    with ExitStack() as ctx:
+        keep = ctx.enter_context(tc.tile_pool(name="keep", bufs=1))
+        psum = ctx.enter_context(tc.psum_pool(name="psum", bufs=1))
+
+        offsets = keep.tile([P, S // 16], U16, name="offsets")
+        nc.sync.dma_start(offsets[:], offs)
+
+        raw = []
+        for i in range(2 * PASSES):
+            t0 = 0
+            row = []
+            for c, (width, share) in enumerate(CHUNKS[i]):
+                chunk = keep.tile([P, 2, width], F32, name=f"raw{i}_{c}")
+                nc.sync.dma_start(chunk[:], planes[i // 2, i % 2, :, :, t0 : t0 + width])
+                row.append((t0, width, share, chunk))
+                t0 += width
+            raw.append(row)
+
+        bias = keep.tile([P, E], F32, name="bias")
+        nc.sync.dma_start(bias[:], b)
+        w_sc = keep.tile([P, E * PASSES, N], U8, name="w_sc", align_bytes=64)
+        nc.vector.memset(w_sc[:].rearrange("p a n -> p (a n)").bitcast(I32), 0)
+        for i in range(4):
+            nc.sync.dma_start(w_sc[i:P:32, :, :].bitcast(I32), scales_hbm[i].bitcast(I32))
+        w_codes = [keep.tile([P, 2 * PASSES, 4 * N], U8, name=f"w_codes{s}", align_bytes=64) for s in range(4)]
+        gates = [keep.tile([P, 512], F32, name=f"gates{h}") for h in range(2)]
+        for s in range(4):
+            nc.sync.dma_start(w_codes[s][:], words_hbm[:, 6 * s : 6 * s + 6, :])
+            if s % 2 == 0:
+                nc.sync.dma_start(gates[s // 2][:], gate[:, 256 * s : 256 * s + 512])
+
+        warm = keep.tile([P, 1], F32, name="warm")
+        nc.vector.memset(warm[:], 0.0)
+        nc.scalar.activation(warm[:], warm[:], GELU)
+        window = keep.tile([P, T], F32, name="window")
+        nc.vector.memset(window[:], 0.0)
+
+        grouped = [keep.tile([P, S, 4], BF16, name=f"grouped{g}", align_bytes=64) for g in range(PASSES)]
+        x_codes = [keep.tile([P, S], U32, name=f"x_codes{g}", align_bytes=64) for g in range(PASSES)]
+        x_sc = [keep.tile([P, S], U8, name=f"x_sc{g}", align_bytes=64) for g in range(PASSES)]
+
+        def gather(i, pair, lo, hi):
+            words = grouped[i // 2][:].rearrange("p s k -> p (s k)").bitcast(U32).rearrange("p (s u) -> p s u", u=2)
+            nc.vector.tensor_copy(
+                words[:, lo:hi, i % 2],
+                pair[:].rearrange("p t j -> p (t j)").bitcast(U32).indirect(offsets[:, lo // 16 : hi // 16]),
+            )
+
+        def quantize(g, lo, hi):
+            nc.vector.quantize_mx(
+                out=x_codes[g][:, lo:hi].bitcast(FP8X4),
+                scales=x_sc[g][:, lo:hi],
+                in_=grouped[g][:, lo:hi, :].rearrange("p s k -> p (s k)"),
+            )
+
+        for i in range(2 * PASSES):
+            pair = keep.tile([P, T, 2], BF16, name=f"pair{i}")
+            for t0, width, share, chunk in raw[i]:
+                nc.scalar.copy(pair[:, t0 : t0 + share, :], chunk[:, :, :share].rearrange("p j t -> p t j"))
+                nc.vector.tensor_copy(pair[:, t0 + share : t0 + width, :], chunk[:, :, share:].rearrange("p j t -> p t j"))
+            if i < 5:
+                gather(i, pair, 0, S)
+                if i % 2 == 1:
+                    quantize(i // 2, 0, S)
+            else:
+                for s in range(4):
+                    gather(i, pair, SLICE * s, SLICE * (s + 1))
+                    if s > 0:
+                        quantize(2, SLICE * (s - 1), SLICE * s)
+                quantize(2, S - SLICE, S)
+
+        sums = [psum.tile([P, C], F32, name=f"sums{e}") for e in range(E)]
+
+        def multiply(e, a):
+            nc.tensor.matmul_mx(
+                out=sums[e][:],
+                lhsT=w_codes[e // 2][:, (e % 2) * PASSES + a, :].bitcast(FP8X4),
+                lhsT_scale=w_sc[:, e * PASSES + a, :],
+                rhs=x_codes[a][:, e * C : (e + 1) * C].bitcast(FP8X4),
+                rhs_scale=x_sc[a][:, e * C : (e + 1) * C],
+                start=(a == 0),
+                stop=(a == PASSES - 1),
+            )
+
+        y = keep.tile([P, S], F32, name="y")
+        scaled = keep.tile([P, S], F32, name="scaled")
+        for s in range(4):
+            lo, hi = SLICE * s, SLICE * (s + 1)
+            for a in range(PASSES - 1):
+                for e in (2 * s, 2 * s + 1):
+                    multiply(e, a)
+            for e in (2 * s, 2 * s + 1):
+                multiply(e, PASSES - 1)
+                nc.scalar.activation(y[:, e * C : (e + 1) * C], sums[e][:], GELU, bias=bias[:, e : e + 1])
+            nc.gpsimd.tensor_tensor(scaled[:, lo:hi], y[:, lo:hi], gates[s // 2][:, lo % 512 : lo % 512 + SLICE], MULT)
+            nc.vector.tensor_copy(window[:].indirect(offsets[:, lo // 16 : hi // 16]), scaled[:, lo:hi])
+        nc.sync.dma_start(out, window[:])

@@ -21,18 +21,16 @@ S = E * C
 
 CHUNKS = [
     [(512, 384), (512, 384), (1024, 768)],
-    [(2048, 1600)],
-    [(2048, 1600)],
-    [(2048, 1600)],
     [(1024, 768), (1024, 768)],
-    [(1024, 768), (512, 320), (256, 96), (256, 96)],
-]
-SLICE = 256
+    [(1024, 768), (512, 384), (256, 128), (256, 128)],
+];
+SLICES = [(0, 512), (512, 1024)]
+SCATTERS = [(0, 256), (256, 512), (512, 768), (768, 1024)]
 
 
 def tile_routed_moe_kernel(tc, xT, w_words, w_scales, b, gate, offs, out):
     nc = tc.nc
-    planes = xT.rearrange("(g p u j) t -> g u p j t", g=PASSES, p=P, u=2, j=2)
+    rows = xT.rearrange("(g p j) t -> g p j t", g=PASSES, p=P, j=4)
     words_hbm = w_words.rearrange("e a p n r -> p (e a) (n r)")
     scales_hbm = w_scales.rearrange("e a (q i) n -> i q (e a) n", i=4)
 
@@ -43,93 +41,89 @@ def tile_routed_moe_kernel(tc, xT, w_words, w_scales, b, gate, offs, out):
         offsets = keep.tile([P, S // 16], U16, name="offsets")
         nc.sync.dma_start(offsets[:], offs)
 
-        raw = []
-        for i in range(2 * PASSES):
-            t0 = 0
-            row = []
-            for c, (width, share) in enumerate(CHUNKS[i]):
-                chunk = keep.tile([P, 2, width], F32, name=f"raw{i}_{c}")
-                nc.sync.dma_start(chunk[:], planes[i // 2, i % 2, :, :, t0 : t0 + width])
-                row.append((t0, width, share, chunk))
-                t0 += width
-            raw.append(row)
-
-        bias = keep.tile([P, E], F32, name="bias")
-        nc.sync.dma_start(bias[:], b)
         w_sc = keep.tile([P, E * PASSES, N], U8, name="w_sc", align_bytes=64)
         nc.vector.memset(w_sc[:].rearrange("p a n -> p (a n)").bitcast(I32), 0)
-        for i in range(4):
-            nc.sync.dma_start(w_sc[i:P:32, :, :].bitcast(I32), scales_hbm[i].bitcast(I32))
-        w_codes = [keep.tile([P, 2 * PASSES, 4 * N], U8, name=f"w_codes{s}", align_bytes=64) for s in range(4)]
-        gates = [keep.tile([P, 512], F32, name=f"gates{h}") for h in range(2)]
-        for s in range(4):
-            nc.sync.dma_start(w_codes[s][:], words_hbm[:, 6 * s : 6 * s + 6, :])
-            if s % 2 == 0:
-                nc.sync.dma_start(gates[s // 2][:], gate[:, 256 * s : 256 * s + 512])
-
         warm = keep.tile([P, 1], F32, name="warm")
         nc.vector.memset(warm[:], 0.0)
         nc.scalar.activation(warm[:], warm[:], GELU)
         window = keep.tile([P, T], F32, name="window")
         nc.vector.memset(window[:], 0.0)
 
-        grouped = [keep.tile([P, S, 4], BF16, name=f"grouped{g}", align_bytes=64) for g in range(PASSES)]
-        x_codes = [keep.tile([P, S], U32, name=f"x_codes{g}", align_bytes=64) for g in range(PASSES)]
-        x_sc = [keep.tile([P, S], U8, name=f"x_sc{g}", align_bytes=64) for g in range(PASSES)]
+        raw = []
+        for a in range(PASSES):
+            t0 = 0
+            row = []
+            for c, (width, share) in enumerate(CHUNKS[a]):
+                chunk = keep.tile([P, 4, width], F32, name=f"raw{a}_{c}")
+                nc.sync.dma_start(chunk[:], rows[a, :, :, t0 : t0 + width])
+                row.append((t0, width, share, chunk))
+                t0 += width
+            raw.append(row)
 
-        def gather(i, pair, lo, hi):
-            words = grouped[i // 2][:].rearrange("p s k -> p (s k)").bitcast(U32).rearrange("p (s u) -> p s u", u=2)
-            nc.vector.tensor_copy(
-                words[:, lo:hi, i % 2],
-                pair[:].rearrange("p t j -> p (t j)").bitcast(U32).indirect(offsets[:, lo // 16 : hi // 16]),
+        bias = keep.tile([P, E], F32, name="bias")
+        nc.sync.dma_start(bias[:], b)
+        for i in range(4):
+            nc.sync.dma_start(w_sc[i:P:32, :, :].bitcast(I32), scales_hbm[i].bitcast(I32))
+        w_codes = [keep.tile([P, 4 * PASSES, 4 * N], U8, name=f"w_codes{h}", align_bytes=64) for h in range(2)]
+        gates = keep.tile([P, S], F32, name="gates")
+        nc.sync.dma_start(w_codes[0][:], words_hbm[:, :12, :])
+        nc.sync.dma_start(gates[:], gate)
+        nc.sync.dma_start(w_codes[1][:], words_hbm[:, 12:, :])
+
+        t_codes = [keep.tile([P, T], U32, name=f"t_codes{a}", align_bytes=64) for a in range(PASSES)]
+        t_sc = keep.tile([P, T], U8, name="t_sc", align_bytes=64)
+        x_sc = keep.tile([P, S], U8, name="x_sc", align_bytes=64)
+        x_codes = [keep.tile([P, S], U32, name=f"x_codes{a}", align_bytes=64) for a in range(PASSES)]
+
+        def cast(copy, grouped, chunk, lo, hi):
+            copy(
+                grouped[:, lo:hi, :].rearrange("p (c i) j -> p c j i", i=4),
+                chunk[:, :, lo:hi].rearrange("p j (c i) -> p c j i", i=4),
             )
 
-        def quantize(g, lo, hi):
-            nc.vector.quantize_mx(
-                out=x_codes[g][:, lo:hi].bitcast(FP8X4),
-                scales=x_sc[g][:, lo:hi],
-                in_=grouped[g][:, lo:hi, :].rearrange("p s k -> p (s k)"),
-            )
+        def gather(dst, table, lo, hi):
+            nc.vector.tensor_copy(dst[:, lo:hi], table[:].indirect(offsets[:, lo // 16 : hi // 16]))
 
-        for i in range(2 * PASSES):
-            pair = keep.tile([P, T, 2], BF16, name=f"pair{i}")
-            for t0, width, share, chunk in raw[i]:
-                nc.scalar.copy(pair[:, t0 : t0 + share, :], chunk[:, :, :share].rearrange("p j t -> p t j"))
-                nc.vector.tensor_copy(pair[:, t0 + share : t0 + width, :], chunk[:, :, share:].rearrange("p j t -> p t j"))
-            if i < 5:
-                gather(i, pair, 0, S)
-                if i % 2 == 1:
-                    quantize(i // 2, 0, S)
-            else:
-                for s in range(4):
-                    gather(i, pair, SLICE * s, SLICE * (s + 1))
-                    if s > 0:
-                        quantize(2, SLICE * (s - 1), SLICE * s)
-                quantize(2, S - SLICE, S)
+        for a in range(PASSES):
+            for c, (t0, width, share, chunk) in enumerate(raw[a]):
+                grouped = keep.tile([P, width, 4], BF16, name=f"grouped{a}_{c}", align_bytes=64)
+                if share < width:
+                    cast(nc.vector.tensor_copy, grouped, chunk, share, width)
+                if share > 0:
+                    cast(nc.scalar.copy, grouped, chunk, 0, share)
+                for q0 in range(0, width, 512):
+                    q1 = min(q0 + 512, width)
+                    nc.vector.quantize_mx(
+                        out=t_codes[a][:, t0 + q0 : t0 + q1].bitcast(FP8X4),
+                        scales=t_sc[4 * a : P, t0 + q0 : t0 + q1],
+                        in_=grouped[:, q0:q1, :].rearrange("p t j -> p (t j)"),
+                    )
+            if a < PASSES - 1:
+                gather(x_codes[a], t_codes[a], 0, S)
+
+        for lo, hi in SLICES:
+            gather(x_codes[PASSES - 1], t_codes[PASSES - 1], lo, hi)
+            gather(x_sc, t_sc, lo, hi)
 
         sums = [psum.tile([P, C], F32, name=f"sums{e}") for e in range(E)]
 
         def multiply(e, a):
             nc.tensor.matmul_mx(
                 out=sums[e][:],
-                lhsT=w_codes[e // 2][:, (e % 2) * PASSES + a, :].bitcast(FP8X4),
+                lhsT=w_codes[e // 4][:, (e % 4) * PASSES + a, :].bitcast(FP8X4),
                 lhsT_scale=w_sc[:, e * PASSES + a, :],
                 rhs=x_codes[a][:, e * C : (e + 1) * C].bitcast(FP8X4),
-                rhs_scale=x_sc[a][:, e * C : (e + 1) * C],
+                rhs_scale=x_sc[4 * a : P, e * C : (e + 1) * C],
                 start=(a == 0),
                 stop=(a == PASSES - 1),
             )
 
         y = keep.tile([P, S], F32, name="y")
-        scaled = keep.tile([P, S], F32, name="scaled")
-        for s in range(4):
-            lo, hi = SLICE * s, SLICE * (s + 1)
-            for a in range(PASSES - 1):
-                for e in (2 * s, 2 * s + 1):
+
+        for lo, hi in SCATTERS:
+            for e in range(lo // C, hi // C):
+                for a in range(PASSES):
                     multiply(e, a)
-            for e in (2 * s, 2 * s + 1):
-                multiply(e, PASSES - 1)
                 nc.scalar.activation(y[:, e * C : (e + 1) * C], sums[e][:], GELU, bias=bias[:, e : e + 1])
-            nc.gpsimd.tensor_tensor(scaled[:, lo:hi], y[:, lo:hi], gates[s // 2][:, lo % 512 : lo % 512 + SLICE], MULT)
-            nc.vector.tensor_copy(window[:].indirect(offsets[:, lo // 16 : hi // 16]), scaled[:, lo:hi])
+            nc.vector.tensor_tensor(window[:].indirect(offsets[:, lo // 16 : hi // 16]), y[:, lo:hi], gates[:, lo:hi], MULT)
         nc.sync.dma_start(out, window[:])

@@ -22,9 +22,9 @@ S = E * C
 CHUNKS = [
     [(512, 384), (512, 384), (1024, 768)],
     [(1024, 768), (1024, 768)],
-    [(1024, 768), (512, 384), (256, 128), (256, 128)],
+    [(1024, 736), (512, 352), (256, 96), (256, 96)],
 ];
-SLICES = [(0, 512), (512, 1024)]
+SLICES = [(0, 512), (512, 768), (768, 1024)]
 SCATTERS = [(0, 256), (256, 512), (512, 768), (768, 1024)]
 
 
@@ -62,13 +62,15 @@ def tile_routed_moe_kernel(tc, xT, w_words, w_scales, b, gate, offs, out):
 
         bias = keep.tile([P, E], F32, name="bias")
         nc.sync.dma_start(bias[:], b)
-        for i in range(4):
-            nc.sync.dma_start(w_sc[i:P:32, :, :].bitcast(I32), scales_hbm[i].bitcast(I32))
         w_codes = [keep.tile([P, 4 * PASSES, 4 * N], U8, name=f"w_codes{h}", align_bytes=64) for h in range(2)]
         gates = keep.tile([P, S], F32, name="gates")
-        nc.sync.dma_start(w_codes[0][:], words_hbm[:, :12, :])
-        nc.sync.dma_start(gates[:], gate)
-        nc.sync.dma_start(w_codes[1][:], words_hbm[:, 12:, :])
+        for h in range(2):
+            half = slice(12 * h, 12 * h + 12)
+            for i in range(4):
+                nc.sync.dma_start(w_sc[i:P:32, half, :].bitcast(I32), scales_hbm[i, :, half, :].bitcast(I32))
+            nc.sync.dma_start(w_codes[h][:], words_hbm[:, half, :])
+            if h == 0:
+                nc.sync.dma_start(gates[:], gate)
 
         t_codes = [keep.tile([P, T], U32, name=f"t_codes{a}", align_bytes=64) for a in range(PASSES)]
         t_sc = keep.tile([P, T], U8, name="t_sc", align_bytes=64)
@@ -119,11 +121,12 @@ def tile_routed_moe_kernel(tc, xT, w_words, w_scales, b, gate, offs, out):
             )
 
         y = keep.tile([P, S], F32, name="y")
-
+        scaled = keep.tile([P, S], F32, name="scaled")
         for lo, hi in SCATTERS:
             for e in range(lo // C, hi // C):
                 for a in range(PASSES):
                     multiply(e, a)
                 nc.scalar.activation(y[:, e * C : (e + 1) * C], sums[e][:], GELU, bias=bias[:, e : e + 1])
-            nc.vector.tensor_tensor(window[:].indirect(offsets[:, lo // 16 : hi // 16]), y[:, lo:hi], gates[:, lo:hi], MULT)
+            nc.gpsimd.tensor_tensor(scaled[:, lo:hi], y[:, lo:hi], gates[:, lo:hi], MULT)
+            nc.vector.tensor_copy(window[:].indirect(offsets[:, lo // 16 : hi // 16]), scaled[:, lo:hi])
         nc.sync.dma_start(out, window[:])

@@ -20,12 +20,12 @@ PASSES = K // 512
 S = E * C
 
 CHUNKS = [
-    [(512, 384), (512, 384), (1024, 768)],
-    [(1024, 768), (1024, 768)],
-    [(1024, 736), (512, 352), (256, 96), (256, 96)],
+    [[("V", 128), ("S", 256), ("S", 128)]] * 4,
+    [[("V", 128), ("S", 256), ("S", 128)]] * 4,
+    [[("V", 128), ("S", 256), ("S", 128)]] * 2 + [[("V", 256), ("S", 256)]] + [[("V", 128), ("S", 128)]] * 2,
 ];
-SLICES = [(0, 512), (512, 768), (768, 1024)]
-SCATTERS = [(0, 256), (256, 512), (512, 768), (768, 1024)]
+SLICES = [(0, 512), (512, 1024)]
+SCATTERS = [(0, 512), (512, 1024)]
 
 
 def tile_routed_moe_kernel(tc, xT, w_words, w_scales, b, gate, offs, out):
@@ -39,7 +39,6 @@ def tile_routed_moe_kernel(tc, xT, w_words, w_scales, b, gate, offs, out):
         psum = ctx.enter_context(tc.psum_pool(name="psum", bufs=1))
 
         offsets = keep.tile([P, S // 16], U16, name="offsets")
-        nc.sync.dma_start(offsets[:], offs)
 
         w_sc = keep.tile([P, E * PASSES, N], U8, name="w_sc", align_bytes=64)
         nc.vector.memset(w_sc[:].rearrange("p a n -> p (a n)").bitcast(I32), 0)
@@ -53,10 +52,13 @@ def tile_routed_moe_kernel(tc, xT, w_words, w_scales, b, gate, offs, out):
         for a in range(PASSES):
             t0 = 0
             row = []
-            for c, (width, share) in enumerate(CHUNKS[a]):
+            for c, pieces in enumerate(CHUNKS[a]):
+                width = sum(n for who, n in pieces)
                 chunk = keep.tile([P, 4, width], F32, name=f"raw{a}_{c}")
                 nc.sync.dma_start(chunk[:], rows[a, :, :, t0 : t0 + width])
-                row.append((t0, width, share, chunk))
+                if a == 0 and c == 0:
+                    nc.sync.dma_start(offsets[:], offs)
+                row.append((t0, pieces, chunk))
                 t0 += width
             raw.append(row)
 
@@ -69,36 +71,36 @@ def tile_routed_moe_kernel(tc, xT, w_words, w_scales, b, gate, offs, out):
             for i in range(4):
                 nc.sync.dma_start(w_sc[i:P:32, half, :].bitcast(I32), scales_hbm[i, :, half, :].bitcast(I32))
             nc.sync.dma_start(w_codes[h][:], words_hbm[:, half, :])
-            if h == 0:
-                nc.sync.dma_start(gates[:], gate)
+            nc.sync.dma_start(gates[:, 512 * h : 512 * h + 512], gate[:, 512 * h : 512 * h + 512])
 
         t_codes = [keep.tile([P, T], U32, name=f"t_codes{a}", align_bytes=64) for a in range(PASSES)]
         t_sc = keep.tile([P, T], U8, name="t_sc", align_bytes=64)
         x_sc = keep.tile([P, S], U8, name="x_sc", align_bytes=64)
         x_codes = [keep.tile([P, S], U32, name=f"x_codes{a}", align_bytes=64) for a in range(PASSES)]
 
-        def cast(copy, grouped, chunk, lo, hi):
+        def cast(copy, grouped, chunk, lo, n):
             copy(
-                grouped[:, lo:hi, :].rearrange("p (c i) j -> p c j i", i=4),
-                chunk[:, :, lo:hi].rearrange("p j (c i) -> p c j i", i=4),
+                grouped[:].rearrange("p (c i) j -> p c j i", i=4),
+                chunk[:, :, lo : lo + n].rearrange("p j (c i) -> p c j i", i=4),
             )
 
         def gather(dst, table, lo, hi):
             nc.vector.tensor_copy(dst[:, lo:hi], table[:].indirect(offsets[:, lo // 16 : hi // 16]))
 
         for a in range(PASSES):
-            for c, (t0, width, share, chunk) in enumerate(raw[a]):
-                grouped = keep.tile([P, width, 4], BF16, name=f"grouped{a}_{c}", align_bytes=64)
-                if share < width:
-                    cast(nc.vector.tensor_copy, grouped, chunk, share, width)
-                if share > 0:
-                    cast(nc.scalar.copy, grouped, chunk, 0, share)
-                for q0 in range(0, width, 512):
-                    q1 = min(q0 + 512, width)
+            for c, (t0, pieces, chunk) in enumerate(raw[a]):
+                todo = []
+                lo = 0
+                for who, n in pieces:
+                    grouped = keep.tile([P, n, 4], BF16, name=f"grouped{a}_{c}_{lo}", align_bytes=64)
+                    cast(nc.scalar.copy if who == "S" else nc.vector.tensor_copy, grouped, chunk, lo, n)
+                    todo.append((lo, n, grouped))
+                    lo += n
+                for lo, n, grouped in todo:
                     nc.vector.quantize_mx(
-                        out=t_codes[a][:, t0 + q0 : t0 + q1].bitcast(FP8X4),
-                        scales=t_sc[4 * a : P, t0 + q0 : t0 + q1],
-                        in_=grouped[:, q0:q1, :].rearrange("p t j -> p (t j)"),
+                        out=t_codes[a][:, t0 + lo : t0 + lo + n].bitcast(FP8X4),
+                        scales=t_sc[4 * a : P, t0 + lo : t0 + lo + n],
+                        in_=grouped[:].rearrange("p t j -> p (t j)"),
                     )
             if a < PASSES - 1:
                 gather(x_codes[a], t_codes[a], 0, S)
@@ -121,12 +123,11 @@ def tile_routed_moe_kernel(tc, xT, w_words, w_scales, b, gate, offs, out):
             )
 
         y = keep.tile([P, S], F32, name="y")
-        scaled = keep.tile([P, S], F32, name="scaled")
+
         for lo, hi in SCATTERS:
             for e in range(lo // C, hi // C):
                 for a in range(PASSES):
                     multiply(e, a)
                 nc.scalar.activation(y[:, e * C : (e + 1) * C], sums[e][:], GELU, bias=bias[:, e : e + 1])
-            nc.gpsimd.tensor_tensor(scaled[:, lo:hi], y[:, lo:hi], gates[:, lo:hi], MULT)
-            nc.vector.tensor_copy(window[:].indirect(offsets[:, lo // 16 : hi // 16]), scaled[:, lo:hi])
+            nc.vector.tensor_tensor(window[:].indirect(offsets[:, lo // 16 : hi // 16]), y[:, lo:hi], gates[:, lo:hi], MULT)
         nc.sync.dma_start(out, window[:])

@@ -20,9 +20,9 @@ PASSES = K // 512
 S = E * C
 
 CHUNKS = [
-    [[("V", 128), ("S", 256), ("S", 128)]] * 4,
-    [[("V", 128), ("S", 256), ("S", 128)]] * 4,
-    [[("V", 128), ("S", 256), ("S", 128)]] * 2 + [[("V", 256), ("S", 256)]] + [[("V", 128), ("S", 128)]] * 2,
+    [[("V", 256), ("V", 512), ("S", 512), ("S", 512), ("S", 256)]],
+    [[("V", 256), ("S", 512), ("S", 256)]] + [[("V", 256), ("S", 256)]] * 2,
+    [[("V", 256), ("V", 128), ("S", 512), ("S", 128)], [("V", 256), ("S", 256)]] + [[("V", 128), ("S", 128)]] * 2,
 ];
 SLICES = [(0, 512), (512, 1024)]
 SCATTERS = [(0, 512), (512, 1024)]

from contextlib import ExitStack

import concourse.mybir as mybir

K, T, E, C, N = 1536, 2048, 8, 128, 128
FLOPS = 2 * K * N * E * C

F32 = mybir.dt.float32
BF16 = mybir.dt.bfloat16
U32 = mybir.dt.uint32
I32 = mybir.dt.int32
U16 = mybir.dt.uint16
U8 = mybir.dt.uint8
FP8X4 = mybir.dt.float8_e4m3fn_x4
GELU = mybir.ActivationFunctionType.Gelu_apprx_tanh
MULT = mybir.AluOpType.mult

P = 128
PASSES = K // 512
S = E * C

CHUNKS = [
    [[("V", 256), ("V", 512), ("S", 512), ("S", 512), ("S", 256)]],
    [[("V", 256), ("S", 512), ("S", 256)]] + [[("V", 256), ("S", 256)]] * 2,
    [[("V", 256), ("V", 128), ("S", 512), ("S", 128)], [("V", 256), ("S", 256)]] + [[("V", 128), ("S", 128)]] * 2,
];
SLICES = [(0, 512), (512, 1024)]
SCATTERS = [(0, 512), (512, 1024)]


def tile_routed_moe_kernel(tc, xT, w_words, w_scales, b, gate, offs, out):
    nc = tc.nc
    rows = xT.rearrange("(g p j) t -> g p j t", g=PASSES, p=P, j=4)
    words_hbm = w_words.rearrange("e a p n r -> p (e a) (n r)")
    scales_hbm = w_scales.rearrange("e a (q i) n -> i q (e a) n", i=4)

    with ExitStack() as ctx:
        keep = ctx.enter_context(tc.tile_pool(name="keep", bufs=1))
        psum = ctx.enter_context(tc.psum_pool(name="psum", bufs=1))

        offsets = keep.tile([P, S // 16], U16, name="offsets")

        w_sc = keep.tile([P, E * PASSES, N], U8, name="w_sc", align_bytes=64)
        nc.vector.memset(w_sc[:].rearrange("p a n -> p (a n)").bitcast(I32), 0)
        warm = keep.tile([P, 1], F32, name="warm")
        nc.vector.memset(warm[:], 0.0)
        nc.scalar.activation(warm[:], warm[:], GELU)
        window = keep.tile([P, T], F32, name="window")
        nc.vector.memset(window[:], 0.0)

        raw = []
        for a in range(PASSES):
            t0 = 0
            row = []
            for c, pieces in enumerate(CHUNKS[a]):
                width = sum(n for who, n in pieces)
                chunk = keep.tile([P, 4, width], F32, name=f"raw{a}_{c}")
                nc.sync.dma_start(chunk[:], rows[a, :, :, t0 : t0 + width])
                if a == 0 and c == 0:
                    nc.sync.dma_start(offsets[:], offs)
                row.append((t0, pieces, chunk))
                t0 += width
            raw.append(row)

        bias = keep.tile([P, E], F32, name="bias")
        nc.sync.dma_start(bias[:], b)
        w_codes = [keep.tile([P, 4 * PASSES, 4 * N], U8, name=f"w_codes{h}", align_bytes=64) for h in range(2)]
        gates = keep.tile([P, S], F32, name="gates")
        for h in range(2):
            half = slice(12 * h, 12 * h + 12)
            for i in range(4):
                nc.sync.dma_start(w_sc[i:P:32, half, :].bitcast(I32), scales_hbm[i, :, half, :].bitcast(I32))
            nc.sync.dma_start(w_codes[h][:], words_hbm[:, half, :])
            nc.sync.dma_start(gates[:, 512 * h : 512 * h + 512], gate[:, 512 * h : 512 * h + 512])

        t_codes = [keep.tile([P, T], U32, name=f"t_codes{a}", align_bytes=64) for a in range(PASSES)]
        t_sc = keep.tile([P, T], U8, name="t_sc", align_bytes=64)
        x_sc = keep.tile([P, S], U8, name="x_sc", align_bytes=64)
        x_codes = [keep.tile([P, S], U32, name=f"x_codes{a}", align_bytes=64) for a in range(PASSES)]

        def cast(copy, grouped, chunk, lo, n):
            copy(
                grouped[:].rearrange("p (c i) j -> p c j i", i=4),
                chunk[:, :, lo : lo + n].rearrange("p j (c i) -> p c j i", i=4),
            )

        def gather(dst, table, lo, hi):
            nc.vector.tensor_copy(dst[:, lo:hi], table[:].indirect(offsets[:, lo // 16 : hi // 16]))

        for a in range(PASSES):
            for c, (t0, pieces, chunk) in enumerate(raw[a]):
                todo = []
                lo = 0
                for who, n in pieces:
                    grouped = keep.tile([P, n, 4], BF16, name=f"grouped{a}_{c}_{lo}", align_bytes=64)
                    cast(nc.scalar.copy if who == "S" else nc.vector.tensor_copy, grouped, chunk, lo, n)
                    todo.append((lo, n, grouped))
                    lo += n
                for lo, n, grouped in todo:
                    nc.vector.quantize_mx(
                        out=t_codes[a][:, t0 + lo : t0 + lo + n].bitcast(FP8X4),
                        scales=t_sc[4 * a : P, t0 + lo : t0 + lo + n],
                        in_=grouped[:].rearrange("p t j -> p (t j)"),
                    )
            if a < PASSES - 1:
                gather(x_codes[a], t_codes[a], 0, S)

        for lo, hi in SLICES:
            gather(x_codes[PASSES - 1], t_codes[PASSES - 1], lo, hi)
            gather(x_sc, t_sc, lo, hi)

        sums = [psum.tile([P, C], F32, name=f"sums{e}") for e in range(E)]

        def multiply(e, a):
            nc.tensor.matmul_mx(
                out=sums[e][:],
                lhsT=w_codes[e // 4][:, (e % 4) * PASSES + a, :].bitcast(FP8X4),
                lhsT_scale=w_sc[:, e * PASSES + a, :],
                rhs=x_codes[a][:, e * C : (e + 1) * C].bitcast(FP8X4),
                rhs_scale=x_sc[4 * a : P, e * C : (e + 1) * C],
                start=(a == 0),
                stop=(a == PASSES - 1),
            )

        y = keep.tile([P, S], F32, name="y")

        for lo, hi in SCATTERS:
            for e in range(lo // C, hi // C):
                for a in range(PASSES):
                    multiply(e, a)
                nc.scalar.activation(y[:, e * C : (e + 1) * C], sums[e][:], GELU, bias=bias[:, e : e + 1])
            nc.vector.tensor_tensor(window[:].indirect(offsets[:, lo // 16 : hi // 16]), y[:, lo:hi], gates[:, lo:hi], MULT)
        nc.sync.dma_start(out, window[:])
